import numpy as np
import ml_dtypes


def mxq(x, axis, fmt="e4m3"):
    dtype, down = {"e4m3": (ml_dtypes.float8_e4m3fn, 7), "e5m2": (ml_dtypes.float8_e5m2, 14)}[fmt]
    v = np.moveaxis(np.asarray(x, np.float32).astype(ml_dtypes.bfloat16).astype(np.float64), axis, -1)
    blocks = v.reshape(v.shape[:-1] + (-1, 32))
    amax = np.abs(blocks).max(-1, keepdims=True)
    byte = np.maximum(np.where(amax > 0, np.frexp(amax)[1] - 1 + 127, 0) - down, 1)
    scale = np.exp2(byte - 127.0)
    codes = (blocks / scale).astype(np.float32).astype(dtype).astype(np.float64)
    return np.moveaxis((codes * scale).reshape(v.shape), -1, axis)


WIDE = False


def mx_kscale(k):
    if not WIDE:
        return np.ones(k)
    levels = np.array([10, -10, 5, -5, 0])
    if k % 512:
        return np.exp2(np.random.permutation(np.resize(levels, k // 32))).repeat(32)
    a = np.empty((k // 512, 16))
    for p in range(k // 512):
        a[p, :8] = np.random.permutation(np.resize(levels, 8))
        for g in range(8):
            far = levels[np.abs(levels - a[p, g]) >= 10]
            a[p, g + 8] = far[np.random.randint(len(far))]
    return np.exp2(a.ravel()).repeat(32)


def f64(x):
    return np.asarray(x).astype(np.float64)


def striped(idx):
    return np.tile(idx.reshape(-1, 16).T, (8, 1)).astype(np.uint16)


def unstriped(offs):
    return offs[:16].T.reshape(-1).astype(np.int64)


def pack_weight(w):
    k, n = w.shape
    w = f64(np.asarray(w, np.float32).astype(ml_dtypes.bfloat16)).reshape(k // 32, 32, n)
    amax = np.abs(w).max(1)
    byte = np.clip(np.where(amax > 0, np.frexp(amax)[1] - 1 + 127 - 7, 1), 1, 254)
    scaled = (w * np.exp2(127.0 - byte)[:, None, :]).reshape(k, n).astype(np.float32)
    words = np.ascontiguousarray(scaled.reshape(k // 512, 128, 4, n).transpose(0, 1, 3, 2)).astype(ml_dtypes.float8_e4m3fn).view(np.uint8)
    return words, np.ascontiguousarray(byte.astype(np.uint8).reshape(k // 512, 16, n))


def unpack_weight(words, scales):
    g, p, n, _ = words.shape
    vals = np.ascontiguousarray(words).view(ml_dtypes.float8_e4m3fn).astype(np.float64) * np.repeat(np.exp2(scales.astype(np.float64) - 127.0), 8, axis=1)[..., None]
    return vals.transpose(0, 1, 3, 2).reshape(g * 512, n)


def sigmoid(v):
    return 1.0 / (1.0 + np.exp(-np.maximum(v, -700.0)))


K, T, S, D, N = 512, 2048, 512, 2, 128


def setup_inputs():
    n = np.random.standard_normal
    s = mx_kscale(K)[:, None]
    packed_xT = pack_weight(n((K, T)) * s)
    return {
        "x_words": packed_xT[0],
        "x_scales": packed_xT[1],
        "w1": (n((K, N)) / np.sqrt(K) / s).astype(np.float32),
        "w2": (n((K, N)) / np.sqrt(K) / s).astype(np.float32),
        "offs": striped(np.random.permutation(T)[:S]),
        "away": striped(np.random.permutation(T)[:S]),
    }


def reference(x_words, x_scales, w1, w2, offs, away):
    xq = unpack_weight(x_words, x_scales)[:, unstriped(offs)]
    w1q = mxq(f64(w1), 0, "e4m3")
    y1 = w1q.T @ xq
    w2q = mxq(f64(w2), 0, "e4m3")
    s1 = np.exp(0.5 * (w2q.T @ xq))
    x_away = unpack_weight(x_words, x_scales)[:, unstriped(away)]
    y2 = w1q.T @ x_away
    s2 = np.exp(0.5 * (w2q.T @ x_away))
    sc = np.sqrt(s1.reshape(len(s1), -1, D).sum(axis=2) + s2.reshape(len(s2), -1, D).sum(axis=2) + 1.0)
    t0 = (y1.reshape(len(y1), -1, D).sum(axis=2) - (y2.reshape(len(y2), -1, D).sum(axis=2))) / sc
    vv = (0.3989 * (np.exp(-0.5 * ((t0) ** 2)))) / (sigmoid(1.702 * t0) + 0.02)
    return y1 + s1 * np.repeat(vv / sc, D, axis=1)

@@ -1,0 +1,133 @@
+import math
+from contextlib import ExitStack
+
+import concourse.mybir as mybir
+
+K, T, S, D, M = 512, 2048, 512, 2, 128
+V = S // D
+P = 128
+PACK = 4
+FLOPS = 4 * 2 * K * M * S
+
+F32 = mybir.dt.float32
+BF16 = mybir.dt.bfloat16
+I32 = mybir.dt.int32
+U32 = mybir.dt.uint32
+U16 = mybir.dt.uint16
+U8 = mybir.dt.uint8
+FP8X4 = mybir.dt.float8_e4m3fn_x4
+ACT = mybir.ActivationFunctionType
+ALU = mybir.AluOpType
+AX = mybir.AxisListType
+
+HALF = S // 2
+TANH_BIAS = 0.5 * math.log(51.0)
+TANH_SHIFT = 1.04
+GAIN = -0.3989 * 1250.0 / 51.0
+
+
+def tile_picked_yskill_mean_p_kernel(tc, x_words, x_scales, w1, w2, offs, away, out):
+    nc = tc.nc
+    with ExitStack() as ctx:
+        sb = ctx.enter_context(tc.tile_pool(name="sb", bufs=1))
+        ps = ctx.enter_context(tc.psum_pool(name="ps", bufs=1))
+
+        offs_sb = sb.tile([P, S // 16], U16, name="offs_sb")
+        away_sb = sb.tile([P, S // 16], U16, name="away_sb")
+        word_table = sb.tile([P, T], U32, name="word_table", align_bytes=64)
+        scale_table = sb.tile([P, T], U8, name="scale_table", align_bytes=64)
+        w1_raw = sb.tile([P, PACK, M], F32, name="w1_raw")
+        w2_raw = sb.tile([P, PACK, M], F32, name="w2_raw")
+
+        nc.vector.memset(scale_table[:].bitcast(I32), 0)
+        nc.sync.dma_start(offs_sb[:], offs)
+        nc.sync.dma_start(away_sb[:], away)
+        scale_rows = x_scales[0].bitcast(I32)
+        for q in range(4):
+            nc.sync.dma_start(scale_table[32 * q : 32 * q + 4, :].bitcast(I32), scale_rows[4 * q : 4 * q + 4, :])
+        nc.sync.dma_start(w2_raw[:], w2.rearrange("(p j) m -> p j m", j=PACK))
+        nc.sync.dma_start(word_table[:].bitcast(I32), x_words[0].rearrange("p n t -> p (n t)").bitcast(I32))
+        nc.sync.dma_start(w1_raw[:], w1.rearrange("(p j) m -> p j m", j=PACK))
+
+        def cast(raw, name):
+            grouped = sb.tile([P, M, PACK], BF16, name=name, align_bytes=64)
+            nc.scalar.activation(grouped[:], raw[:].rearrange("p j m -> p m j"), ACT.Copy)
+            return grouped
+
+        def quantize(grouped, name):
+            codes = sb.tile([P, M], U32, name=name + "_codes", align_bytes=64)
+            scales = sb.tile([P, M], U8, name=name + "_scales", align_bytes=64)
+            nc.vector.quantize_mx(out=codes[:].bitcast(FP8X4), scales=scales[:], in_=grouped[:].rearrange("p m j -> p (m j)"))
+            return codes, scales
+
+        def product(weights, words, scales, name):
+            acc = ps.tile([P, words.shape[1]], F32, name=name)
+            nc.tensor.matmul_mx(out=acc[:], lhsT=weights[0][:].bitcast(FP8X4), lhsT_scale=weights[1][:],
+                                rhs=words.bitcast(FP8X4), rhs_scale=scales, start=True, stop=True)
+            return acc
+
+        win_scales = sb.tile([P, S], U8, name="win_scales", align_bytes=64)
+        lose_scales = sb.tile([P, S], U8, name="lose_scales", align_bytes=64)
+        win_words = sb.tile([P, S], U32, name="win_words", align_bytes=64)
+        lose_words = sb.tile([P, S], U32, name="lose_words", align_bytes=64)
+
+        nc.vector.tensor_copy(win_scales[:], scale_table[:].indirect(offs_sb[:]))
+        nc.vector.tensor_copy(lose_scales[:], scale_table[:].indirect(away_sb[:]))
+        w2q = quantize(cast(w2_raw, "w2_bf"), "w2")
+        w1_bf = cast(w1_raw, "w1_bf")
+
+        s1 = sb.tile([P, S], F32, name="s1")
+        s2 = sb.tile([P, S], F32, name="s2")
+        nc.vector.tensor_copy(win_words[:], word_table[:].indirect(offs_sb[:]))
+        z1 = product(w2q, win_words[:], win_scales[:], "z1")
+        nc.scalar.activation(s1[:], z1[:], ACT.Exp, scale=0.5)
+        for h in range(2):
+            cols = slice(h * HALF, (h + 1) * HALF)
+            nc.vector.tensor_copy(lose_words[:, cols], word_table[:].indirect(away_sb[:, h * HALF // 16 : (h + 1) * HALF // 16]))
+            z2 = product(w2q, lose_words[:, cols], lose_scales[:, cols], "z2_%d" % h)
+            nc.scalar.activation(s2[:, cols], z2[:], ACT.Exp, scale=0.5)
+
+        w1q = quantize(w1_bf, "w1")
+        y1 = product(w1q, win_words[:], win_scales[:], "y1")
+        y2 = product(w1q, lose_words[:], lose_scales[:], "y2")
+
+        def small(name):
+            return sb.tile([P, V], F32, name=name)
+
+        sum_a, sum_b, total = small("sum_a"), small("sum_b"), small("total")
+        nc.vector.tensor_tensor(sum_a[:], s1[:, 0::2], s1[:, 1::2], ALU.add)
+        nc.vector.tensor_tensor(sum_b[:], s2[:, 0::2], s2[:, 1::2], ALU.add)
+        nc.vector.tensor_tensor(total[:], sum_a[:], sum_b[:], ALU.add)
+        inv_sc = small("inv_sc")
+        nc.scalar.activation(inv_sc[:], total[:], ACT.Abs_reciprocal_sqrt, bias=1.0)
+
+        d0, d1, d2 = small("d0"), small("d1"), small("d2")
+        nc.vector.tensor_reduce(d0[:], y1[:].rearrange("p (v d) -> p v d", d=D), AX.X, ALU.add)
+        nc.vector.tensor_tensor(d1[:], d0[:], y2[:, 0::2], ALU.subtract)
+        nc.vector.tensor_tensor(d2[:], d1[:], y2[:, 1::2], ALU.subtract)
+
+        t0, tsq = small("t0"), small("tsq")
+        nc.vector.tensor_tensor(t0[:], d2[:], inv_sc[:], ALU.mult)
+        s1r = sb.tile([P, V, D], F32, name="s1r")
+        nc.vector.scalar_tensor_tensor(s1r[:], s1[:].rearrange("p (v d) -> p v d", d=D), GAIN,
+                                       inv_sc[:].unsqueeze(2).to_broadcast([P, V, D]), ALU.mult, ALU.mult)
+        nc.vector.tensor_tensor(tsq[:], t0[:], t0[:], ALU.mult)
+
+        gauss, th, coef = small("gauss"), small("th"), small("coef")
+        upd = sb.tile([P, V, D], F32, name="upd")
+        res = sb.tile([P, S], F32, name="res")
+        HV = V // 2
+        for h in range(2):
+            vs = slice(h * HV, (h + 1) * HV)
+            nc.scalar.activation(gauss[:, vs], tsq[:, vs], ACT.Exp, scale=-0.5)
+            nc.scalar.activation(th[:, vs], t0[:, vs], ACT.Tanh, scale=0.851, bias=TANH_BIAS)
+        for h in range(2):
+            vs = slice(h * HV, (h + 1) * HV)
+            nc.vector.scalar_tensor_tensor(coef[:, vs], th[:, vs], TANH_SHIFT, gauss[:, vs], ALU.subtract, ALU.mult)
+        for h in range(2):
+            vs = slice(h * HV, (h + 1) * HV)
+            nc.vector.tensor_tensor(upd[:, vs, :], s1r[:, vs, :], coef[:, vs].unsqueeze(2).to_broadcast([P, HV, D]), ALU.mult)
+        for h in range(2):
+            cols = slice(h * HALF, (h + 1) * HALF)
+            nc.vector.tensor_tensor(res[:, cols], upd[:].rearrange("p v d -> p (v d)")[:, cols], y1[:, cols], ALU.add)
+            nc.sync.dma_start(out[:, cols], res[:, cols])

@@ -39,20 +39,18 @@ def tile_picked_yskill_mean_p_kernel(tc, x_words, x_scales, w1, w2, offs, away, 
         w1_raw = sb.tile([P, PACK, M], F32, name="w1_raw")
         w2_raw = sb.tile([P, PACK, M], F32, name="w2_raw")
 
+        nc.scalar.dma_start(w2_raw[:], w2.rearrange("(p j) m -> p j m", j=PACK))
         nc.vector.memset(scale_table[:].bitcast(I32), 0)
         nc.sync.dma_start(offs_sb[:], offs)
         nc.sync.dma_start(away_sb[:], away)
         scale_rows = x_scales[0].bitcast(I32)
-        for q in range(4):
-            nc.sync.dma_start(scale_table[32 * q : 32 * q + 4, :].bitcast(I32), scale_rows[4 * q : 4 * q + 4, :])
-        nc.sync.dma_start(w2_raw[:], w2.rearrange("(p j) m -> p j m", j=PACK))
+        for r in range(4):
+            nc.sync.dma_start(scale_table[r:P:32, :].bitcast(I32), scale_rows[r:16:4, :])
         nc.sync.dma_start(word_table[:].bitcast(I32), x_words[0].rearrange("p n t -> p (n t)").bitcast(I32))
         nc.sync.dma_start(w1_raw[:], w1.rearrange("(p j) m -> p j m", j=PACK))
 
-        def cast(raw, name):
-            grouped = sb.tile([P, M, PACK], BF16, name=name, align_bytes=64)
-            nc.scalar.activation(grouped[:], raw[:].rearrange("p j m -> p m j"), ACT.Copy)
-            return grouped
+        w1_bf = sb.tile([P, M, PACK], BF16, name="w1_bf", align_bytes=64)
+        w2_bf = sb.tile([P, M, PACK], BF16, name="w2_bf", align_bytes=64)
 
         def quantize(grouped, name):
             codes = sb.tile([P, M], U32, name=name + "_codes", align_bytes=64)
@@ -71,10 +69,11 @@ def tile_picked_yskill_mean_p_kernel(tc, x_words, x_scales, w1, w2, offs, away, 
         win_words = sb.tile([P, S], U32, name="win_words", align_bytes=64)
         lose_words = sb.tile([P, S], U32, name="lose_words", align_bytes=64)
 
+        nc.vector.tensor_copy(w2_bf[:], w2_raw[:].rearrange("p j m -> p m j"))
+        w2q = quantize(w2_bf, "w2")
         nc.vector.tensor_copy(win_scales[:], scale_table[:].indirect(offs_sb[:]))
         nc.vector.tensor_copy(lose_scales[:], scale_table[:].indirect(away_sb[:]))
-        w2q = quantize(cast(w2_raw, "w2_bf"), "w2")
-        w1_bf = cast(w1_raw, "w1_bf")
+        nc.scalar.activation(w1_bf[:], w1_raw[:].rearrange("p j m -> p m j"), ACT.Copy)
 
         s1 = sb.tile([P, S], F32, name="s1")
         s2 = sb.tile([P, S], F32, name="s2")
@@ -108,10 +107,10 @@ def tile_picked_yskill_mean_p_kernel(tc, x_words, x_scales, w1, w2, offs, away, 
 
         t0, tsq = small("t0"), small("tsq")
         nc.vector.tensor_tensor(t0[:], d2[:], inv_sc[:], ALU.mult)
+        nc.vector.tensor_tensor(tsq[:], t0[:], t0[:], ALU.mult)
         s1r = sb.tile([P, V, D], F32, name="s1r")
         nc.vector.scalar_tensor_tensor(s1r[:], s1[:].rearrange("p (v d) -> p v d", d=D), GAIN,
                                        inv_sc[:].unsqueeze(2).to_broadcast([P, V, D]), ALU.mult, ALU.mult)
-        nc.vector.tensor_tensor(tsq[:], t0[:], t0[:], ALU.mult)
 
         gauss, th, coef = small("gauss"), small("th"), small("coef")
         upd = sb.tile([P, V, D], F32, name="upd")

@@ -35,7 +35,7 @@ def tile_picked_yskill_mean_p_kernel(tc, x_words, x_scales, w1, w2, offs, away, 
         offs_sb = sb.tile([P, S // 16], U16, name="offs_sb")
         away_sb = sb.tile([P, S // 16], U16, name="away_sb")
         word_table = sb.tile([P, T], U32, name="word_table", align_bytes=64)
-        scale_table = sb.tile([P, T], U8, name="scale_table", align_bytes=64)
+        scale_table = sb.tile([P, T], U8, name="scale_table", tag="scale_table", align_bytes=64)
         w1_raw = sb.tile([P, PACK, M], F32, name="w1_raw")
         w2_raw = sb.tile([P, PACK, M], F32, name="w2_raw")
 
@@ -52,8 +52,8 @@ def tile_picked_yskill_mean_p_kernel(tc, x_words, x_scales, w1, w2, offs, away, 
         w1_bf = sb.tile([P, M, PACK], BF16, name="w1_bf", align_bytes=64)
         w2_bf = sb.tile([P, M, PACK], BF16, name="w2_bf", align_bytes=64)
 
-        def quantize(grouped, name):
-            codes = sb.tile([P, M], U32, name=name + "_codes", align_bytes=64)
+        def quantize(grouped, name, tag):
+            codes = sb.tile([P, M], U32, name=name + "_codes", tag=tag, align_bytes=64)
             scales = sb.tile([P, M], U8, name=name + "_scales", align_bytes=64)
             nc.vector.quantize_mx(out=codes[:].bitcast(FP8X4), scales=scales[:], in_=grouped[:].rearrange("p m j -> p (m j)"))
             return codes, scales
@@ -70,23 +70,24 @@ def tile_picked_yskill_mean_p_kernel(tc, x_words, x_scales, w1, w2, offs, away, 
         lose_words = sb.tile([P, S], U32, name="lose_words", align_bytes=64)
 
         nc.vector.tensor_copy(w2_bf[:], w2_raw[:].rearrange("p j m -> p m j"))
-        w2q = quantize(w2_bf, "w2")
+        w2q = quantize(w2_bf, "w2", "w2_codes")
         nc.vector.tensor_copy(win_scales[:], scale_table[:].indirect(offs_sb[:]))
         nc.vector.tensor_copy(lose_scales[:], scale_table[:].indirect(away_sb[:]))
         nc.scalar.activation(w1_bf[:], w1_raw[:].rearrange("p j m -> p m j"), ACT.Copy)
 
         s1 = sb.tile([P, S], F32, name="s1")
         s2 = sb.tile([P, S], F32, name="s2")
-        nc.vector.tensor_copy(win_words[:], word_table[:].indirect(offs_sb[:]))
-        z1 = product(w2q, win_words[:], win_scales[:], "z1")
-        nc.scalar.activation(s1[:], z1[:], ACT.Exp, scale=0.5)
-        for h in range(2):
-            cols = slice(h * HALF, (h + 1) * HALF)
-            nc.vector.tensor_copy(lose_words[:, cols], word_table[:].indirect(away_sb[:, h * HALF // 16 : (h + 1) * HALF // 16]))
-            z2 = product(w2q, lose_words[:, cols], lose_scales[:, cols], "z2_%d" % h)
-            nc.scalar.activation(s2[:, cols], z2[:], ACT.Exp, scale=0.5)
+        for team, (entries, words, scales, s) in enumerate(((offs_sb, win_words, win_scales, s1), (away_sb, lose_words, lose_scales, s2))):
+            for h in range(2):
+                cols = slice(h * HALF, (h + 1) * HALF)
+                nc.vector.tensor_copy(words[:, cols], word_table[:].indirect(entries[:, h * HALF // 16 : (h + 1) * HALF // 16]))
+                width = HALF // 2 if (team, h) == (1, 1) else HALF
+                for c0 in range(h * HALF, (h + 1) * HALF, width):
+                    part = slice(c0, c0 + width)
+                    z = product(w2q, words[:, part], scales[:, part], "z%d_%d" % (team, c0))
+                    nc.scalar.activation(s[:, part], z[:], ACT.Exp, scale=0.5)
 
-        w1q = quantize(w1_bf, "w1")
+        w1q = quantize(w1_bf, "w1", "w1_codes")
         y1 = product(w1q, win_words[:], win_scales[:], "y1")
         y2 = product(w1q, lose_words[:], lose_scales[:], "y2")
 
@@ -95,22 +96,38 @@ def tile_picked_yskill_mean_p_kernel(tc, x_words, x_scales, w1, w2, offs, away, 
 
         sum_a, sum_b, total = small("sum_a"), small("sum_b"), small("total")
         nc.vector.tensor_tensor(sum_a[:], s1[:, 0::2], s1[:, 1::2], ALU.add)
-        nc.vector.tensor_tensor(sum_b[:], s2[:, 0::2], s2[:, 1::2], ALU.add)
-        nc.vector.tensor_tensor(total[:], sum_a[:], sum_b[:], ALU.add)
+        s2_pairs = s2[:].rearrange("p (v d) -> p v d", d=D)
+        for h in range(2):
+            vs = slice(h * V // 2, (h + 1) * V // 2)
+            nc.vector.tensor_tensor(sum_b[:, vs], sum_a[:, vs], s2_pairs[:, vs, 0], ALU.add)
+            nc.vector.tensor_tensor(total[:, vs], sum_b[:, vs], s2_pairs[:, vs, 1], ALU.add)
         inv_sc = small("inv_sc")
         nc.scalar.activation(inv_sc[:], total[:], ACT.Abs_reciprocal_sqrt, bias=1.0)
 
-        d0, d1, d2 = small("d0"), small("d1"), small("d2")
-        nc.vector.tensor_reduce(d0[:], y1[:].rearrange("p (v d) -> p v d", d=D), AX.X, ALU.add)
-        nc.vector.tensor_tensor(d1[:], d0[:], y2[:, 0::2], ALU.subtract)
-        nc.vector.tensor_tensor(d2[:], d1[:], y2[:, 1::2], ALU.subtract)
-
+        d0, d1, d2 = sum_a, small("d1"), small("d2")
         t0, tsq = small("t0"), small("tsq")
-        nc.vector.tensor_tensor(t0[:], d2[:], inv_sc[:], ALU.mult)
-        nc.vector.tensor_tensor(tsq[:], t0[:], t0[:], ALU.mult)
         s1r = sb.tile([P, V, D], F32, name="s1r")
-        nc.vector.scalar_tensor_tensor(s1r[:], s1[:].rearrange("p (v d) -> p v d", d=D), GAIN,
-                                       inv_sc[:].unsqueeze(2).to_broadcast([P, V, D]), ALU.mult, ALU.mult)
+        y1_pairs = y1[:].rearrange("p (v d) -> p v d", d=D)
+        y2_pairs = y2[:].rearrange("p (v d) -> p v d", d=D)
+        halves = [slice(h * V // 2, (h + 1) * V // 2) for h in range(2)]
+        for vs in halves:
+            nc.vector.tensor_reduce(d0[:, vs], y1_pairs[:, vs, :], AX.X, ALU.add)
+        for vs in halves:
+            nc.vector.tensor_tensor(d1[:, vs], d0[:, vs], y2_pairs[:, vs, 0], ALU.subtract)
+        for vs in halves:
+            nc.vector.tensor_tensor(d2[:, vs], d1[:, vs], y2_pairs[:, vs, 1], ALU.subtract)
+        s1_pairs = s1[:].rearrange("p (v d) -> p v d", d=D)
+
+        def scale_variances(vs):
+            nc.vector.scalar_tensor_tensor(s1r[:, vs, :], s1_pairs[:, vs, :], GAIN,
+                                           inv_sc[:, vs].unsqueeze(2).to_broadcast([P, V // 2, D]), ALU.mult, ALU.mult)
+
+        for vs in halves:
+            nc.vector.tensor_tensor(t0[:, vs], d2[:, vs], inv_sc[:, vs], ALU.mult)
+        scale_variances(halves[0])
+        for vs in halves:
+            nc.vector.tensor_tensor(tsq[:, vs], t0[:, vs], t0[:, vs], ALU.mult)
+        scale_variances(halves[1])
 
         gauss, th, coef = small("gauss"), small("th"), small("coef")
         upd = sb.tile([P, V, D], F32, name="upd")
@@ -118,8 +135,8 @@ def tile_picked_yskill_mean_p_kernel(tc, x_words, x_scales, w1, w2, offs, away, 
         HV = V // 2
         for h in range(2):
             vs = slice(h * HV, (h + 1) * HV)
-            nc.scalar.activation(gauss[:, vs], tsq[:, vs], ACT.Exp, scale=-0.5)
             nc.scalar.activation(th[:, vs], t0[:, vs], ACT.Tanh, scale=0.851, bias=TANH_BIAS)
+            nc.scalar.activation(gauss[:, vs], tsq[:, vs], ACT.Exp, scale=-0.5)
         for h in range(2):
             vs = slice(h * HV, (h + 1) * HV)
             nc.vector.scalar_tensor_tensor(coef[:, vs], th[:, vs], TANH_SHIFT, gauss[:, vs], ALU.subtract, ALU.mult)

import math
from contextlib import ExitStack

import concourse.mybir as mybir

K, T, S, D, M = 512, 2048, 512, 2, 128
V = S // D
P = 128
PACK = 4
FLOPS = 4 * 2 * K * M * S

F32 = mybir.dt.float32
BF16 = mybir.dt.bfloat16
I32 = mybir.dt.int32
U32 = mybir.dt.uint32
U16 = mybir.dt.uint16
U8 = mybir.dt.uint8
FP8X4 = mybir.dt.float8_e4m3fn_x4
ACT = mybir.ActivationFunctionType
ALU = mybir.AluOpType
AX = mybir.AxisListType

HALF = S // 2
TANH_BIAS = 0.5 * math.log(51.0)
TANH_SHIFT = 1.04
GAIN = -0.3989 * 1250.0 / 51.0


def tile_picked_yskill_mean_p_kernel(tc, x_words, x_scales, w1, w2, offs, away, out):
    nc = tc.nc
    with ExitStack() as ctx:
        sb = ctx.enter_context(tc.tile_pool(name="sb", bufs=1))
        ps = ctx.enter_context(tc.psum_pool(name="ps", bufs=1))

        offs_sb = sb.tile([P, S // 16], U16, name="offs_sb")
        away_sb = sb.tile([P, S // 16], U16, name="away_sb")
        word_table = sb.tile([P, T], U32, name="word_table", align_bytes=64)
        scale_table = sb.tile([P, T], U8, name="scale_table", tag="scale_table", align_bytes=64)
        w1_raw = sb.tile([P, PACK, M], F32, name="w1_raw")
        w2_raw = sb.tile([P, PACK, M], F32, name="w2_raw")

        nc.scalar.dma_start(w2_raw[:], w2.rearrange("(p j) m -> p j m", j=PACK))
        nc.vector.memset(scale_table[:].bitcast(I32), 0)
        nc.sync.dma_start(offs_sb[:], offs)
        nc.sync.dma_start(away_sb[:], away)
        scale_rows = x_scales[0].bitcast(I32)
        for r in range(4):
            nc.sync.dma_start(scale_table[r:P:32, :].bitcast(I32), scale_rows[r:16:4, :])
        nc.sync.dma_start(word_table[:].bitcast(I32), x_words[0].rearrange("p n t -> p (n t)").bitcast(I32))
        nc.sync.dma_start(w1_raw[:], w1.rearrange("(p j) m -> p j m", j=PACK))

        w1_bf = sb.tile([P, M, PACK], BF16, name="w1_bf", align_bytes=64)
        w2_bf = sb.tile([P, M, PACK], BF16, name="w2_bf", align_bytes=64)

        def quantize(grouped, name, tag):
            codes = sb.tile([P, M], U32, name=name + "_codes", tag=tag, align_bytes=64)
            scales = sb.tile([P, M], U8, name=name + "_scales", align_bytes=64)
            nc.vector.quantize_mx(out=codes[:].bitcast(FP8X4), scales=scales[:], in_=grouped[:].rearrange("p m j -> p (m j)"))
            return codes, scales

        def product(weights, words, scales, name):
            acc = ps.tile([P, words.shape[1]], F32, name=name)
            nc.tensor.matmul_mx(out=acc[:], lhsT=weights[0][:].bitcast(FP8X4), lhsT_scale=weights[1][:],
                                rhs=words.bitcast(FP8X4), rhs_scale=scales, start=True, stop=True)
            return acc

        win_scales = sb.tile([P, S], U8, name="win_scales", align_bytes=64)
        lose_scales = sb.tile([P, S], U8, name="lose_scales", align_bytes=64)
        win_words = sb.tile([P, S], U32, name="win_words", align_bytes=64)
        lose_words = sb.tile([P, S], U32, name="lose_words", align_bytes=64)

        nc.vector.tensor_copy(w2_bf[:], w2_raw[:].rearrange("p j m -> p m j"))
        w2q = quantize(w2_bf, "w2", "w2_codes")
        nc.vector.tensor_copy(win_scales[:], scale_table[:].indirect(offs_sb[:]))
        nc.vector.tensor_copy(lose_scales[:], scale_table[:].indirect(away_sb[:]))
        nc.scalar.activation(w1_bf[:], w1_raw[:].rearrange("p j m -> p m j"), ACT.Copy)

        s1 = sb.tile([P, S], F32, name="s1")
        s2 = sb.tile([P, S], F32, name="s2")
        for team, (entries, words, scales, s) in enumerate(((offs_sb, win_words, win_scales, s1), (away_sb, lose_words, lose_scales, s2))):
            for h in range(2):
                cols = slice(h * HALF, (h + 1) * HALF)
                nc.vector.tensor_copy(words[:, cols], word_table[:].indirect(entries[:, h * HALF // 16 : (h + 1) * HALF // 16]))
                width = HALF // 2 if (team, h) == (1, 1) else HALF
                for c0 in range(h * HALF, (h + 1) * HALF, width):
                    part = slice(c0, c0 + width)
                    z = product(w2q, words[:, part], scales[:, part], "z%d_%d" % (team, c0))
                    nc.scalar.activation(s[:, part], z[:], ACT.Exp, scale=0.5)

        w1q = quantize(w1_bf, "w1", "w1_codes")
        y1 = product(w1q, win_words[:], win_scales[:], "y1")
        y2 = product(w1q, lose_words[:], lose_scales[:], "y2")

        def small(name):
            return sb.tile([P, V], F32, name=name)

        sum_a, sum_b, total = small("sum_a"), small("sum_b"), small("total")
        nc.vector.tensor_tensor(sum_a[:], s1[:, 0::2], s1[:, 1::2], ALU.add)
        s2_pairs = s2[:].rearrange("p (v d) -> p v d", d=D)
        for h in range(2):
            vs = slice(h * V // 2, (h + 1) * V // 2)
            nc.vector.tensor_tensor(sum_b[:, vs], sum_a[:, vs], s2_pairs[:, vs, 0], ALU.add)
            nc.vector.tensor_tensor(total[:, vs], sum_b[:, vs], s2_pairs[:, vs, 1], ALU.add)
        inv_sc = small("inv_sc")
        nc.scalar.activation(inv_sc[:], total[:], ACT.Abs_reciprocal_sqrt, bias=1.0)

        d0, d1, d2 = sum_a, small("d1"), small("d2")
        t0, tsq = small("t0"), small("tsq")
        s1r = sb.tile([P, V, D], F32, name="s1r")
        y1_pairs = y1[:].rearrange("p (v d) -> p v d", d=D)
        y2_pairs = y2[:].rearrange("p (v d) -> p v d", d=D)
        halves = [slice(h * V // 2, (h + 1) * V // 2) for h in range(2)]
        for vs in halves:
            nc.vector.tensor_reduce(d0[:, vs], y1_pairs[:, vs, :], AX.X, ALU.add)
        for vs in halves:
            nc.vector.tensor_tensor(d1[:, vs], d0[:, vs], y2_pairs[:, vs, 0], ALU.subtract)
        for vs in halves:
            nc.vector.tensor_tensor(d2[:, vs], d1[:, vs], y2_pairs[:, vs, 1], ALU.subtract)
        s1_pairs = s1[:].rearrange("p (v d) -> p v d", d=D)

        def scale_variances(vs):
            nc.vector.scalar_tensor_tensor(s1r[:, vs, :], s1_pairs[:, vs, :], GAIN,
                                           inv_sc[:, vs].unsqueeze(2).to_broadcast([P, V // 2, D]), ALU.mult, ALU.mult)

        for vs in halves:
            nc.vector.tensor_tensor(t0[:, vs], d2[:, vs], inv_sc[:, vs], ALU.mult)
        scale_variances(halves[0])
        for vs in halves:
            nc.vector.tensor_tensor(tsq[:, vs], t0[:, vs], t0[:, vs], ALU.mult)
        scale_variances(halves[1])

        gauss, th, coef = small("gauss"), small("th"), small("coef")
        upd = sb.tile([P, V, D], F32, name="upd")
        res = sb.tile([P, S], F32, name="res")
        HV = V // 2
        for h in range(2):
            vs = slice(h * HV, (h + 1) * HV)
            nc.scalar.activation(th[:, vs], t0[:, vs], ACT.Tanh, scale=0.851, bias=TANH_BIAS)
            nc.scalar.activation(gauss[:, vs], tsq[:, vs], ACT.Exp, scale=-0.5)
        for h in range(2):
            vs = slice(h * HV, (h + 1) * HV)
            nc.vector.scalar_tensor_tensor(coef[:, vs], th[:, vs], TANH_SHIFT, gauss[:, vs], ALU.subtract, ALU.mult)
        for h in range(2):
            vs = slice(h * HV, (h + 1) * HV)
            nc.vector.tensor_tensor(upd[:, vs, :], s1r[:, vs, :], coef[:, vs].unsqueeze(2).to_broadcast([P, HV, D]), ALU.mult)
        for h in range(2):
            cols = slice(h * HALF, (h + 1) * HALF)
            nc.vector.tensor_tensor(res[:, cols], upd[:].rearrange("p v d -> p (v d)")[:, cols], y1[:, cols], ALU.add)
            nc.sync.dma_start(out[:, cols], res[:, cols])
